import numpy as np
import ml_dtypes


def mxq(x, axis, fmt="e4m3"):
    dtype, down = {"e4m3": (ml_dtypes.float8_e4m3fn, 7), "e5m2": (ml_dtypes.float8_e5m2, 14)}[fmt]
    v = np.moveaxis(np.asarray(x, np.float32).astype(ml_dtypes.bfloat16).astype(np.float64), axis, -1)
    blocks = v.reshape(v.shape[:-1] + (-1, 32))
    amax = np.abs(blocks).max(-1, keepdims=True)
    byte = np.maximum(np.where(amax > 0, np.frexp(amax)[1] - 1 + 127, 0) - down, 1)
    scale = np.exp2(byte - 127.0)
    codes = (blocks / scale).astype(np.float32).astype(dtype).astype(np.float64)
    return np.moveaxis((codes * scale).reshape(v.shape), -1, axis)


WIDE = False


def mx_kscale(k):
    if not WIDE:
        return np.ones(k)
    levels = np.array([10, -10, 5, -5, 0])
    if k % 512:
        return np.exp2(np.random.permutation(np.resize(levels, k // 32))).repeat(32)
    a = np.empty((k // 512, 16))
    for p in range(k // 512):
        a[p, :8] = np.random.permutation(np.resize(levels, 8))
        for g in range(8):
            far = levels[np.abs(levels - a[p, g]) >= 10]
            a[p, g + 8] = far[np.random.randint(len(far))]
    return np.exp2(a.ravel()).repeat(32)


def f64(x):
    return np.asarray(x).astype(np.float64)


def striped(idx):
    return np.tile(idx.reshape(-1, 16).T, (8, 1)).astype(np.uint16)


def unstriped(offs):
    return offs[:16].T.reshape(-1).astype(np.int64)


def striped8(idx):
    return np.concatenate([x.reshape(-1, 16).T for x in idx]).astype(np.uint16)


def runs(offs, k):
    lists = np.stack([offs[16 * r : 16 * r + 16].T.reshape(-1) for r in range(8)]).astype(np.int64)
    return lists[np.arange(k) % 512 // 64]


def pack_weight(w):
    k, n = w.shape
    w = f64(np.asarray(w, np.float32).astype(ml_dtypes.bfloat16)).reshape(k // 32, 32, n)
    amax = np.abs(w).max(1)
    byte = np.clip(np.where(amax > 0, np.frexp(amax)[1] - 1 + 127 - 7, 1), 1, 254)
    scaled = (w * np.exp2(127.0 - byte)[:, None, :]).reshape(k, n).astype(np.float32)
    words = np.ascontiguousarray(scaled.reshape(k // 512, 128, 4, n).transpose(0, 1, 3, 2)).astype(ml_dtypes.float8_e4m3fn).view(np.uint8)
    return words, np.ascontiguousarray(byte.astype(np.uint8).reshape(k // 512, 16, n))


def unpack_weight(words, scales):
    g, p, n, _ = words.shape
    vals = np.ascontiguousarray(words).view(ml_dtypes.float8_e4m3fn).astype(np.float64) * np.repeat(np.exp2(scales.astype(np.float64) - 127.0), 8, axis=1)[..., None]
    return vals.transpose(0, 1, 3, 2).reshape(g * 512, n)


def gelu(v):
    return 0.5 * v * (1.0 + np.tanh(np.sqrt(2.0 / np.pi) * (v + 0.044715 * v**3)))


K, T, S, V, N, H = 512, 2048, 512, 256, 512, 512


def setup_inputs():
    n = np.random.standard_normal
    s = mx_kscale(K)[:, None]
    u = mx_kscale(H)
    packed_xT = pack_weight(n((K, T)) * s)
    return {
        "x_words": packed_xT[0],
        "x_scales": packed_xT[1],
        "w1": (n((K, H)) / np.sqrt(K) / s * u).astype(np.float32),
        "wt": np.repeat(np.random.uniform(0.3, 1.2, (8, V)), 64, axis=0).astype(np.float32),
        "w2": (n((K, H)) / np.sqrt(K) / s * u).astype(np.float32),
        "w3": (n((H, N)) / np.sqrt(2 * H) / u[:, None]).astype(np.float32),
        "w4": (n((H, N)) / np.sqrt(2 * H) / u[:, None]).astype(np.float32),
        "offs": striped(np.random.permutation(T)[:S]),
        "take": striped8(np.stack([np.random.permutation(S)[:V] for _ in range(8)])),
    }


def reference(x_words, x_scales, w1, wt, w2, w3, w4, offs, take):
    xq = unpack_weight(x_words, x_scales)[:, unstriped(offs)]
    y = mxq(f64(w1), 0, "e4m3").T @ xq
    e = (gelu(y[np.arange(H)[:, None], runs(take, H)])) * f64(wt)
    z = np.zeros((H, S))
    z[np.arange(H)[:, None], runs(take, H)] = e
    z2 = gelu(mxq(f64(w2), 0, "e4m3").T @ xq)
    return mxq(f64(w3), 0, "e4m3").T @ mxq(z, 0, "e4m3") + mxq(f64(w4), 0, "e4m3").T @ mxq(z2, 0, "e4m3")

@@ -1,0 +1,211 @@
+from contextlib import ExitStack
+
+import concourse.mybir as mybir
+
+K, T, S, V, N, H = 512, 2048, 512, 256, 512, 512
+FLOPS = 2 * (2 * K * H * S + 2 * H * N * S)
+
+F32 = mybir.dt.float32
+BF16 = mybir.dt.bfloat16
+I32 = mybir.dt.int32
+U32 = mybir.dt.uint32
+U16 = mybir.dt.uint16
+U8 = mybir.dt.uint8
+FP8X4 = mybir.dt.float8_e4m3fn_x4
+GELU = mybir.ActivationFunctionType.Gelu_apprx_tanh
+MULT = mybir.AluOpType.mult
+
+P = 128
+PACK = 4
+HALF = S // 2
+QUARTER = S // 4
+PLANE_ORDER = (1, 2, 3, 0)
+
+
+def tile_picked_sharedexp_gelu_p_kernel(
+    tc, x_words, x_scales, w1, wt, w2, w3, w4, offs, take, out
+):
+    nc = tc.nc
+    with ExitStack() as ctx:
+        sb = ctx.enter_context(tc.tile_pool(name="sb", bufs=1))
+        ps = ctx.enter_context(tc.psum_pool(name="ps", bufs=1))
+
+        def bank(index, shape, name):
+            return ps.tile(shape, F32, name=name, tag="bank%d" % index)
+
+        def quantize(codes, scales, values):
+            nc.vector.quantize_mx(out=codes.bitcast(FP8X4), scales=scales, in_=values)
+
+        def mm(acc, lhs, lhs_cols, rhs, rhs_cols, start, stop):
+            nc.tensor.matmul_mx(
+                out=acc,
+                lhsT=lhs[0][:, lhs_cols].bitcast(FP8X4),
+                lhsT_scale=lhs[1][:, lhs_cols],
+                rhs=rhs[0][:, rhs_cols].bitcast(FP8X4),
+                rhs_scale=rhs[1][:, rhs_cols],
+                start=start,
+                stop=stop,
+            )
+
+        def mx_operand(name, width):
+            codes = sb.tile([P, width], U32, name=name + "_codes", align_bytes=64)
+            scales = sb.tile([P, width], U8, name=name + "_scales", align_bytes=64)
+            return codes, scales
+
+        def cols(index, width):
+            return slice(index * width, (index + 1) * width)
+
+        offs_sb = sb.tile([P, S // 16], U16, name="offs_sb")
+        take_sb = sb.tile([P, V // 16], U16, name="take_sb")
+        xw = sb.tile([P, T], I32, name="xw", align_bytes=64)
+        xs = sb.tile([P, T], U8, name="xs", align_bytes=64)
+        wt_sb = sb.tile([P, V], F32, name="wt_sb")
+        raw = {}
+        for name in ("w1", "w2", "w3", "w4"):
+            raw[name] = sb.tile([P, PACK, H], F32, name=name + "_raw")
+
+        nc.vector.memset(xs[:].bitcast(I32), 0)
+        zero = sb.tile([P, 1], F32, name="zero")
+        nc.vector.memset(zero[:], 0.0)
+
+        nc.sync.dma_start(out=raw["w1"][:], in_=w1.rearrange("(p j) c -> p j c", j=PACK))
+        for quad in range(4):
+            nc.sync.dma_start(
+                out=xs[32 * quad : 32 * quad + 4, :].bitcast(I32),
+                in_=x_scales[0, 4 * quad : 4 * quad + 4, :].bitcast(I32),
+            )
+        nc.sync.dma_start(offs_sb[:], offs)
+        nc.sync.dma_start(out=xw[:], in_=x_words[0].rearrange("p c r -> p (c r)").bitcast(I32))
+        nc.sync.dma_start(take_sb[:], take)
+        nc.sync.dma_start(out=wt_sb[:], in_=wt.rearrange("(p j) v -> p j v", j=PACK)[:, 0, :])
+        nc.sync.dma_start(out=raw["w2"][:], in_=w2.rearrange("(p j) c -> p j c", j=PACK))
+        for name, w in (("w4", w4), ("w3", w3)):
+            rows = w.rearrange("(b t q) c -> t b q c", t=PACK, q=8)
+            for t in range(PACK):
+                nc.sync.dma_start(out=raw[name][:, t, :], in_=rows[t])
+
+        bias0 = sb.tile([P, 1], F32, name="bias0")
+        nc.scalar.activation(out=bias0[:], in_=zero[:], func=GELU)
+
+        wide = sb.tile([P, PACK * S], F32, name="wide")
+        nc.vector.memset(wide[:, 0:S], 0.0)
+        window = {0: wide}
+        for t in PLANE_ORDER[:-1]:
+            window[t] = sb.tile([P, S], F32, name="z%d" % t)
+            nc.vector.memset(window[t][:], 0.0)
+
+        def cast_first_layer(engine_copy, name, t, staged):
+            src = raw[name][:].rearrange("p j (b t h i) -> p t b h j i", t=PACK, h=2, i=4)[:, t]
+            dst = staged.rearrange("p (b h i j) -> p b h j i", h=2, i=4, j=PACK)
+            engine_copy(out=dst, in_=src)
+
+        def interleave(engine_copy, staged, planes):
+            engine_copy(
+                out=staged.rearrange("p (c i t) -> p c t i", i=4, t=PACK),
+                in_=planes.rearrange("p t (c i) -> p c t i", i=4),
+            )
+
+        xq = (
+            sb.tile([P, S], U32, name="xq_codes", align_bytes=64),
+            sb.tile([P, S], U8, name="xq_scales", align_bytes=64),
+        )
+        nc.vector.tensor_copy(xq[1][:], xs[:].indirect(offs_sb[:]))
+
+        w1q = mx_operand("w1q", H)
+        for t in PLANE_ORDER:
+            staged = sb.tile([P, P * PACK], BF16, name="w1s%d" % t, align_bytes=64)
+            cast_first_layer(nc.vector.tensor_copy if t == PLANE_ORDER[0] else nc.scalar.copy, "w1", t, staged[:])
+            quantize(w1q[0][:, cols(t, P)], w1q[1][:, cols(t, P)], staged[:])
+
+        for h in range(2):
+            nc.vector.tensor_copy(
+                xq[0][:, cols(h, HALF)], xw[:].bitcast(U32).indirect(offs_sb[:, cols(h, HALF // 16)])
+            )
+
+        act = {}
+        for n, t in enumerate(PLANE_ORDER):
+            act[t] = sb.tile([P, S], F32, name="act%d" % t)
+            pieces = 2 if n == 0 else 1
+            width = S // pieces
+            for h in range(pieces):
+                acc = bank(h if n == 0 else n + 1, [P, width], "y%d_%d" % (t, h))
+                mm(acc[:], w1q, cols(t, P), xq, cols(h, width), True, True)
+                nc.scalar.activation(out=act[t][:, cols(h, width)], in_=acc[:], func=GELU, bias=bias0[:])
+
+        picked = {}
+
+        def gather(t, tag):
+            picked[t] = sb.tile([P, V], F32, name="picked%d" % t, tag=tag, align_bytes=64)
+            nc.vector.tensor_copy(picked[t][:], act[t][:].indirect(take_sb[:]))
+
+        def scatter(t):
+            nc.vector.tensor_tensor(window[t][:].indirect(take_sb[:]), picked[t][:], wt_sb[:], MULT)
+
+        gather(1, "picked1")
+        gather(2, "picked2")
+        scatter(1)
+        nc.sync.dma_start(out=wide[:, cols(1, S)], in_=window[1][:])
+        scatter(2)
+        nc.sync.dma_start(out=wide[:, cols(2, S)], in_=window[2][:])
+
+        w2s = sb.tile([P, H * PACK], BF16, name="w2s", tag="hold_a", align_bytes=64)
+        for t in range(PACK):
+            cast_first_layer(nc.scalar.copy, "w2", t, w2s[:, cols(t, P * PACK)])
+        w2q = mx_operand("w2q", H)
+        quantize(w2q[0][:], w2q[1][:], w2s[:])
+
+        z2s = sb.tile([P, S * PACK], BF16, name="z2s", tag="hold_b", align_bytes=64)
+        for c in range(4):
+            acc = bank((5 + c) % 8, [P, PACK, QUARTER], "y2_%d" % c)
+            for t in range(PACK):
+                mm(acc[:, t, :], w2q, cols(t, P), xq, cols(c, QUARTER), True, True)
+            nc.scalar.activation(
+                out=z2s[:, cols(c, QUARTER * PACK)].rearrange("p (n t) -> p n t", t=PACK),
+                in_=acc[:].rearrange("p t n -> p n t"),
+                func=GELU,
+                bias=bias0[:],
+            )
+
+        gather(3, "hold_a")
+        scatter(3)
+        nc.scalar.copy(out=wide[:, cols(3, S)], in_=window[3][:])
+
+        second = {}
+        staged_w = {}
+        for name in ("w4", "w3"):
+            staged_w[name] = sb.tile([P, N * PACK], BF16, name=name + "s", align_bytes=64)
+            second[name] = mx_operand(name + "q", N)
+
+        def cast_second_layer(name):
+            for m in range(4):
+                interleave(nc.scalar.copy, staged_w[name][:, cols(m, P * PACK)], raw[name][:, :, cols(m, P)])
+            quantize(second[name][0][:], second[name][1][:], staged_w[name][:])
+
+        cast_second_layer("w4")
+        z2q = mx_operand("z2q", S)
+        quantize(z2q[0][:], z2q[1][:], z2s[:])
+        result = {}
+        for h in range(2):
+            for m in range(4):
+                result[h, m] = bank((1 + 4 * h + m) % 8, [P, HALF], "out%d_%d" % (h, m))
+                mm(result[h, m][:], second["w4"], cols(m, P), z2q, cols(h, HALF), True, False)
+
+        gather(0, "hold_b")
+        cast_second_layer("w3")
+        scatter(0)
+
+        planes = wide[:].rearrange("p (t c) -> p t c", t=PACK)
+        zq = mx_operand("zq", S)
+        for h in range(2):
+            staged = sb.tile([P, HALF * PACK], BF16, name="zs%d" % h, align_bytes=64)
+            interleave(nc.vector.tensor_copy if h == 0 else nc.scalar.copy, staged[:], planes[:, :, cols(h, HALF)])
+            quantize(zq[0][:, cols(h, HALF)], zq[1][:, cols(h, HALF)], staged[:])
+        for h in range(2):
+            for m in range(4):
+                mm(result[h, m][:], second["w3"], cols(m, P), zq, cols(h, HALF), False, True)
+                done = sb.tile([P, HALF], F32, name="done%d_%d" % (h, m))
+                if m % 2 == 0:
+                    nc.scalar.copy(out=done[:], in_=result[h, m][:])
+                else:
+                    nc.vector.tensor_copy(out=done[:], in_=result[h, m][:])
+                nc.sync.dma_start(out=out[cols(m, P), cols(h, HALF)], in_=done[:])

@@ -59,7 +59,7 @@ def tile_picked_sharedexp_gelu_p_kernel(
         take_sb = sb.tile([P, V // 16], U16, name="take_sb")
         xw = sb.tile([P, T], I32, name="xw", align_bytes=64)
         xs = sb.tile([P, T], U8, name="xs", align_bytes=64)
-        wt_sb = sb.tile([P, V], F32, name="wt_sb")
+        wt_sb = [sb.tile([P, V], F32, name="wt%d" % t) for t in range(PACK)]
         raw = {}
         for name in ("w1", "w2", "w3", "w4"):
             raw[name] = sb.tile([P, PACK, H], F32, name=name + "_raw")
@@ -68,21 +68,31 @@ def tile_picked_sharedexp_gelu_p_kernel(
         zero = sb.tile([P, 1], F32, name="zero")
         nc.vector.memset(zero[:], 0.0)
 
-        nc.sync.dma_start(out=raw["w1"][:], in_=w1.rearrange("(p j) c -> p j c", j=PACK))
+        def plane_rows(w, t):
+            return w.rearrange("(b t q) c -> t b q c", t=PACK, q=8)[t]
+
+        def load_gate(t):
+            nc.sync.dma_start(out=wt_sb[t][:], in_=plane_rows(wt, t))
+
+        nc.sync.dma_start(out=xw[:], in_=x_words[0].rearrange("p c r -> p (c r)").bitcast(I32))
+        nc.sync.dma_start(offs_sb[:], offs)
         for quad in range(4):
             nc.sync.dma_start(
                 out=xs[32 * quad : 32 * quad + 4, :].bitcast(I32),
                 in_=x_scales[0, 4 * quad : 4 * quad + 4, :].bitcast(I32),
             )
-        nc.sync.dma_start(offs_sb[:], offs)
-        nc.sync.dma_start(out=xw[:], in_=x_words[0].rearrange("p c r -> p (c r)").bitcast(I32))
+        nc.sync.dma_start(out=raw["w1"][:], in_=w1.rearrange("(p j) c -> p j c", j=PACK))
         nc.sync.dma_start(take_sb[:], take)
-        nc.sync.dma_start(out=wt_sb[:], in_=wt.rearrange("(p j) v -> p j v", j=PACK)[:, 0, :])
         nc.sync.dma_start(out=raw["w2"][:], in_=w2.rearrange("(p j) c -> p j c", j=PACK))
-        for name, w in (("w4", w4), ("w3", w3)):
-            rows = w.rearrange("(b t q) c -> t b q c", t=PACK, q=8)
-            for t in range(PACK):
-                nc.sync.dma_start(out=raw[name][:, t, :], in_=rows[t])
+        for t in range(PACK):
+            nc.sync.dma_start(out=raw["w4"][:, t, :], in_=plane_rows(w4, t))
+            if t == 0:
+                load_gate(1)
+        load_gate(2)
+        load_gate(3)
+        for t in range(PACK):
+            nc.sync.dma_start(out=raw["w3"][:, t, :], in_=plane_rows(w3, t))
+        load_gate(0)
 
         bias0 = sb.tile([P, 1], F32, name="bias0")
         nc.scalar.activation(out=bias0[:], in_=zero[:], func=GELU)
@@ -109,54 +119,56 @@ def tile_picked_sharedexp_gelu_p_kernel(
             sb.tile([P, S], U32, name="xq_codes", align_bytes=64),
             sb.tile([P, S], U8, name="xq_scales", align_bytes=64),
         )
+        nc.vector.tensor_copy(xq[0][:], xw[:].bitcast(U32).indirect(offs_sb[:]))
         nc.vector.tensor_copy(xq[1][:], xs[:].indirect(offs_sb[:]))
 
         w1q = mx_operand("w1q", H)
         for t in PLANE_ORDER:
             staged = sb.tile([P, P * PACK], BF16, name="w1s%d" % t, align_bytes=64)
-            cast_first_layer(nc.vector.tensor_copy if t == PLANE_ORDER[0] else nc.scalar.copy, "w1", t, staged[:])
+            cast_first_layer(nc.scalar.copy if t == PLANE_ORDER[1] else nc.vector.tensor_copy, "w1", t, staged[:])
             quantize(w1q[0][:, cols(t, P)], w1q[1][:, cols(t, P)], staged[:])
 
-        for h in range(2):
-            nc.vector.tensor_copy(
-                xq[0][:, cols(h, HALF)], xw[:].bitcast(U32).indirect(offs_sb[:, cols(h, HALF // 16)])
-            )
-
         act = {}
+        first = {}
         for n, t in enumerate(PLANE_ORDER):
             act[t] = sb.tile([P, S], F32, name="act%d" % t)
-            pieces = 2 if n == 0 else 1
+            pieces = 4 if n == 0 else 1
             width = S // pieces
             for h in range(pieces):
-                acc = bank(h if n == 0 else n + 1, [P, width], "y%d_%d" % (t, h))
+                acc = bank(h if n == 0 else n + 3, [P, width], "y%d_%d" % (t, h))
                 mm(acc[:], w1q, cols(t, P), xq, cols(h, width), True, True)
-                nc.scalar.activation(out=act[t][:, cols(h, width)], in_=acc[:], func=GELU, bias=bias0[:])
+                first[t, h] = acc
 
         picked = {}
 
-        def gather(t, tag):
-            picked[t] = sb.tile([P, V], F32, name="picked%d" % t, tag=tag, align_bytes=64)
+        def activate_and_gather(t):
+            pieces = 4 if t == PLANE_ORDER[0] else 1
+            for h in range(pieces):
+                nc.scalar.activation(out=act[t][:, cols(h, S // pieces)], in_=first[t, h][:], func=GELU, bias=bias0[:])
+            picked[t] = sb.tile([P, V], F32, name="picked%d" % t)
             nc.vector.tensor_copy(picked[t][:], act[t][:].indirect(take_sb[:]))
 
         def scatter(t):
-            nc.vector.tensor_tensor(window[t][:].indirect(take_sb[:]), picked[t][:], wt_sb[:], MULT)
+            nc.vector.tensor_tensor(window[t][:].indirect(take_sb[:]), picked[t][:], wt_sb[t][:], MULT)
 
-        gather(1, "picked1")
-        gather(2, "picked2")
+        for t in PLANE_ORDER[:3]:
+            activate_and_gather(t)
         scatter(1)
         nc.sync.dma_start(out=wide[:, cols(1, S)], in_=window[1][:])
-        scatter(2)
-        nc.sync.dma_start(out=wide[:, cols(2, S)], in_=window[2][:])
 
-        w2s = sb.tile([P, H * PACK], BF16, name="w2s", tag="hold_a", align_bytes=64)
+        w2s = sb.tile([P, H * PACK], BF16, name="w2s", align_bytes=64)
         for t in range(PACK):
             cast_first_layer(nc.scalar.copy, "w2", t, w2s[:, cols(t, P * PACK)])
         w2q = mx_operand("w2q", H)
         quantize(w2q[0][:], w2q[1][:], w2s[:])
+        activate_and_gather(0)
+        scatter(2)
+        nc.sync.dma_start(out=wide[:, cols(2, S)], in_=window[2][:])
+        scatter(3)
 
-        z2s = sb.tile([P, S * PACK], BF16, name="z2s", tag="hold_b", align_bytes=64)
+        z2s = sb.tile([P, S * PACK], BF16, name="z2s", align_bytes=64)
         for c in range(4):
-            acc = bank((5 + c) % 8, [P, PACK, QUARTER], "y2_%d" % c)
+            acc = bank((7 + c) % 8, [P, PACK, QUARTER], "y2_%d" % c)
             for t in range(PACK):
                 mm(acc[:, t, :], w2q, cols(t, P), xq, cols(c, QUARTER), True, True)
             nc.scalar.activation(
@@ -165,10 +177,6 @@ def tile_picked_sharedexp_gelu_p_kernel(
                 func=GELU,
                 bias=bias0[:],
             )
-
-        gather(3, "hold_a")
-        scatter(3)
-        nc.scalar.copy(out=wide[:, cols(3, S)], in_=window[3][:])
 
         second = {}
         staged_w = {}
@@ -179,27 +187,38 @@ def tile_picked_sharedexp_gelu_p_kernel(
         def cast_second_layer(name):
             for m in range(4):
                 interleave(nc.scalar.copy, staged_w[name][:, cols(m, P * PACK)], raw[name][:, :, cols(m, P)])
-            quantize(second[name][0][:], second[name][1][:], staged_w[name][:])
 
-        cast_second_layer("w4")
+        def quantize_w3(h):
+            width = N // 2
+            quantize(
+                second["w3"][0][:, cols(h, width)],
+                second["w3"][1][:, cols(h, width)],
+                staged_w["w3"][:, cols(h, width * PACK)],
+            )
+
         z2q = mx_operand("z2q", S)
         quantize(z2q[0][:], z2q[1][:], z2s[:])
+        cast_second_layer("w4")
+        quantize(second["w4"][0][:], second["w4"][1][:], staged_w["w4"][:])
         result = {}
         for h in range(2):
             for m in range(4):
-                result[h, m] = bank((1 + 4 * h + m) % 8, [P, HALF], "out%d_%d" % (h, m))
+                result[h, m] = bank((3 + 4 * h + m) % 8, [P, HALF], "out%d_%d" % (h, m))
                 mm(result[h, m][:], second["w4"], cols(m, P), z2q, cols(h, HALF), True, False)
 
-        gather(0, "hold_b")
-        cast_second_layer("w3")
+        nc.scalar.copy(out=wide[:, cols(3, S)], in_=window[3][:])
         scatter(0)
+        cast_second_layer("w3")
 
         planes = wide[:].rearrange("p (t c) -> p t c", t=PACK)
         zq = mx_operand("zq", S)
-        for h in range(2):
-            staged = sb.tile([P, HALF * PACK], BF16, name="zs%d" % h, align_bytes=64)
-            interleave(nc.vector.tensor_copy if h == 0 else nc.scalar.copy, staged[:], planes[:, :, cols(h, HALF)])
-            quantize(zq[0][:, cols(h, HALF)], zq[1][:, cols(h, HALF)], staged[:])
+        zs = [sb.tile([P, HALF * PACK], BF16, name="zs%d" % h, align_bytes=64) for h in range(2)]
+        interleave(nc.vector.tensor_copy, zs[0][:], planes[:, :, 0:HALF])
+        interleave(nc.scalar.copy, zs[1][:], planes[:, :, HALF:S])
+        quantize_w3(0)
+        quantize(zq[0][:, cols(0, HALF)], zq[1][:, cols(0, HALF)], zs[0][:])
+        quantize_w3(1)
+        quantize(zq[0][:, cols(1, HALF)], zq[1][:, cols(1, HALF)], zs[1][:])
         for h in range(2):
             for m in range(4):
                 mm(result[h, m][:], second["w3"], cols(m, P), zq, cols(h, HALF), False, True)

@@ -81,8 +81,8 @@ def tile_picked_sharedexp_gelu_p_kernel(
                 out=xs[32 * quad : 32 * quad + 4, :].bitcast(I32),
                 in_=x_scales[0, 4 * quad : 4 * quad + 4, :].bitcast(I32),
             )
-        nc.sync.dma_start(out=raw["w1"][:], in_=w1.rearrange("(p j) c -> p j c", j=PACK))
         nc.sync.dma_start(take_sb[:], take)
+        nc.sync.dma_start(out=raw["w1"][:], in_=w1.rearrange("(p j) c -> p j c", j=PACK))
         nc.sync.dma_start(out=raw["w2"][:], in_=w2.rearrange("(p j) c -> p j c", j=PACK))
         for t in range(PACK):
             nc.sync.dma_start(out=raw["w4"][:, t, :], in_=plane_rows(w4, t))
@@ -132,17 +132,17 @@ def tile_picked_sharedexp_gelu_p_kernel(
         first = {}
         for n, t in enumerate(PLANE_ORDER):
             act[t] = sb.tile([P, S], F32, name="act%d" % t)
-            pieces = 4 if n == 0 else 1
+            pieces = 2 if n == 0 else 1
             width = S // pieces
             for h in range(pieces):
-                acc = bank(h if n == 0 else n + 3, [P, width], "y%d_%d" % (t, h))
+                acc = bank(h if n == 0 else n + 1, [P, width], "y%d_%d" % (t, h))
                 mm(acc[:], w1q, cols(t, P), xq, cols(h, width), True, True)
                 first[t, h] = acc
 
         picked = {}
 
         def activate_and_gather(t):
-            pieces = 4 if t == PLANE_ORDER[0] else 1
+            pieces = 2 if t == PLANE_ORDER[0] else 1
             for h in range(pieces):
                 nc.scalar.activation(out=act[t][:, cols(h, S // pieces)], in_=first[t, h][:], func=GELU, bias=bias0[:])
             picked[t] = sb.tile([P, V], F32, name="picked%d" % t)
@@ -168,7 +168,7 @@ def tile_picked_sharedexp_gelu_p_kernel(
 
         z2s = sb.tile([P, S * PACK], BF16, name="z2s", align_bytes=64)
         for c in range(4):
-            acc = bank((7 + c) % 8, [P, PACK, QUARTER], "y2_%d" % c)
+            acc = bank((5 + c) % 8, [P, PACK, QUARTER], "y2_%d" % c)
             for t in range(PACK):
                 mm(acc[:, t, :], w2q, cols(t, P), xq, cols(c, QUARTER), True, True)
             nc.scalar.activation(
@@ -203,7 +203,7 @@ def tile_picked_sharedexp_gelu_p_kernel(
         result = {}
         for h in range(2):
             for m in range(4):
-                result[h, m] = bank((3 + 4 * h + m) % 8, [P, HALF], "out%d_%d" % (h, m))
+                result[h, m] = bank((1 + 4 * h + m) % 8, [P, HALF], "out%d_%d" % (h, m))
                 mm(result[h, m][:], second["w4"], cols(m, P), z2q, cols(h, HALF), True, False)
 
         nc.scalar.copy(out=wide[:, cols(3, S)], in_=window[3][:])
@@ -219,12 +219,15 @@ def tile_picked_sharedexp_gelu_p_kernel(
         quantize(zq[0][:, cols(0, HALF)], zq[1][:, cols(0, HALF)], zs[0][:])
         quantize_w3(1)
         quantize(zq[0][:, cols(1, HALF)], zq[1][:, cols(1, HALF)], zs[1][:])
-        for h in range(2):
-            for m in range(4):
+        done = [sb.tile([P, S], F32, name="done%d" % m) for m in range(4)]
+        for h, order in ((0, (0, 1, 2, 3)), (1, (2, 3, 0, 1))):
+            for m in order:
                 mm(result[h, m][:], second["w3"], cols(m, P), zq, cols(h, HALF), False, True)
-                done = sb.tile([P, HALF], F32, name="done%d_%d" % (h, m))
                 if m % 2 == 0:
-                    nc.scalar.copy(out=done[:], in_=result[h, m][:])
+                    nc.scalar.copy(out=done[m][:, cols(h, HALF)], in_=result[h, m][:])
                 else:
-                    nc.vector.tensor_copy(out=done[:], in_=result[h, m][:])
-                nc.sync.dma_start(out=out[cols(m, P), cols(h, HALF)], in_=done[:])
+                    nc.vector.tensor_copy(out=done[m][:, cols(h, HALF)], in_=result[h, m][:])
+                if m < 2:
+                    nc.sync.dma_start(out=out[cols(m, P), cols(h, HALF)], in_=done[m][:, cols(h, HALF)])
+                elif h == 1:
+                    nc.sync.dma_start(out=out[cols(m, P), :], in_=done[m][:])

from contextlib import ExitStack

import concourse.mybir as mybir

K, T, S, V, N, H = 512, 2048, 512, 256, 512, 512
FLOPS = 2 * (2 * K * H * S + 2 * H * N * S)

F32 = mybir.dt.float32
BF16 = mybir.dt.bfloat16
I32 = mybir.dt.int32
U32 = mybir.dt.uint32
U16 = mybir.dt.uint16
U8 = mybir.dt.uint8
FP8X4 = mybir.dt.float8_e4m3fn_x4
GELU = mybir.ActivationFunctionType.Gelu_apprx_tanh
MULT = mybir.AluOpType.mult

P = 128
PACK = 4
HALF = S // 2
QUARTER = S // 4
PLANE_ORDER = (1, 2, 3, 0)


def tile_picked_sharedexp_gelu_p_kernel(
    tc, x_words, x_scales, w1, wt, w2, w3, w4, offs, take, out
):
    nc = tc.nc
    with ExitStack() as ctx:
        sb = ctx.enter_context(tc.tile_pool(name="sb", bufs=1))
        ps = ctx.enter_context(tc.psum_pool(name="ps", bufs=1))

        def bank(index, shape, name):
            return ps.tile(shape, F32, name=name, tag="bank%d" % index)

        def quantize(codes, scales, values):
            nc.vector.quantize_mx(out=codes.bitcast(FP8X4), scales=scales, in_=values)

        def mm(acc, lhs, lhs_cols, rhs, rhs_cols, start, stop):
            nc.tensor.matmul_mx(
                out=acc,
                lhsT=lhs[0][:, lhs_cols].bitcast(FP8X4),
                lhsT_scale=lhs[1][:, lhs_cols],
                rhs=rhs[0][:, rhs_cols].bitcast(FP8X4),
                rhs_scale=rhs[1][:, rhs_cols],
                start=start,
                stop=stop,
            )

        def mx_operand(name, width):
            codes = sb.tile([P, width], U32, name=name + "_codes", align_bytes=64)
            scales = sb.tile([P, width], U8, name=name + "_scales", align_bytes=64)
            return codes, scales

        def cols(index, width):
            return slice(index * width, (index + 1) * width)

        offs_sb = sb.tile([P, S // 16], U16, name="offs_sb")
        take_sb = sb.tile([P, V // 16], U16, name="take_sb")
        xw = sb.tile([P, T], I32, name="xw", align_bytes=64)
        xs = sb.tile([P, T], U8, name="xs", align_bytes=64)
        wt_sb = [sb.tile([P, V], F32, name="wt%d" % t) for t in range(PACK)]
        raw = {}
        for name in ("w1", "w2", "w3", "w4"):
            raw[name] = sb.tile([P, PACK, H], F32, name=name + "_raw")

        nc.vector.memset(xs[:].bitcast(I32), 0)
        zero = sb.tile([P, 1], F32, name="zero")
        nc.vector.memset(zero[:], 0.0)

        def plane_rows(w, t):
            return w.rearrange("(b t q) c -> t b q c", t=PACK, q=8)[t]

        def load_gate(t):
            nc.sync.dma_start(out=wt_sb[t][:], in_=plane_rows(wt, t))

        nc.sync.dma_start(out=xw[:], in_=x_words[0].rearrange("p c r -> p (c r)").bitcast(I32))
        nc.sync.dma_start(offs_sb[:], offs)
        for quad in range(4):
            nc.sync.dma_start(
                out=xs[32 * quad : 32 * quad + 4, :].bitcast(I32),
                in_=x_scales[0, 4 * quad : 4 * quad + 4, :].bitcast(I32),
            )
        nc.sync.dma_start(take_sb[:], take)
        nc.sync.dma_start(out=raw["w1"][:], in_=w1.rearrange("(p j) c -> p j c", j=PACK))
        nc.sync.dma_start(out=raw["w2"][:], in_=w2.rearrange("(p j) c -> p j c", j=PACK))
        for t in range(PACK):
            nc.sync.dma_start(out=raw["w4"][:, t, :], in_=plane_rows(w4, t))
            if t == 0:
                load_gate(1)
        load_gate(2)
        load_gate(3)
        for t in range(PACK):
            nc.sync.dma_start(out=raw["w3"][:, t, :], in_=plane_rows(w3, t))
        load_gate(0)

        bias0 = sb.tile([P, 1], F32, name="bias0")
        nc.scalar.activation(out=bias0[:], in_=zero[:], func=GELU)

        wide = sb.tile([P, PACK * S], F32, name="wide")
        nc.vector.memset(wide[:, 0:S], 0.0)
        window = {0: wide}
        for t in PLANE_ORDER[:-1]:
            window[t] = sb.tile([P, S], F32, name="z%d" % t)
            nc.vector.memset(window[t][:], 0.0)

        def cast_first_layer(engine_copy, name, t, staged):
            src = raw[name][:].rearrange("p j (b t h i) -> p t b h j i", t=PACK, h=2, i=4)[:, t]
            dst = staged.rearrange("p (b h i j) -> p b h j i", h=2, i=4, j=PACK)
            engine_copy(out=dst, in_=src)

        def interleave(engine_copy, staged, planes):
            engine_copy(
                out=staged.rearrange("p (c i t) -> p c t i", i=4, t=PACK),
                in_=planes.rearrange("p t (c i) -> p c t i", i=4),
            )

        xq = (
            sb.tile([P, S], U32, name="xq_codes", align_bytes=64),
            sb.tile([P, S], U8, name="xq_scales", align_bytes=64),
        )
        nc.vector.tensor_copy(xq[0][:], xw[:].bitcast(U32).indirect(offs_sb[:]))
        nc.vector.tensor_copy(xq[1][:], xs[:].indirect(offs_sb[:]))

        w1q = mx_operand("w1q", H)
        for t in PLANE_ORDER:
            staged = sb.tile([P, P * PACK], BF16, name="w1s%d" % t, align_bytes=64)
            cast_first_layer(nc.scalar.copy if t == PLANE_ORDER[1] else nc.vector.tensor_copy, "w1", t, staged[:])
            quantize(w1q[0][:, cols(t, P)], w1q[1][:, cols(t, P)], staged[:])

        act = {}
        first = {}
        for n, t in enumerate(PLANE_ORDER):
            act[t] = sb.tile([P, S], F32, name="act%d" % t)
            pieces = 2 if n == 0 else 1
            width = S // pieces
            for h in range(pieces):
                acc = bank(h if n == 0 else n + 1, [P, width], "y%d_%d" % (t, h))
                mm(acc[:], w1q, cols(t, P), xq, cols(h, width), True, True)
                first[t, h] = acc

        picked = {}

        def activate_and_gather(t):
            pieces = 2 if t == PLANE_ORDER[0] else 1
            for h in range(pieces):
                nc.scalar.activation(out=act[t][:, cols(h, S // pieces)], in_=first[t, h][:], func=GELU, bias=bias0[:])
            picked[t] = sb.tile([P, V], F32, name="picked%d" % t)
            nc.vector.tensor_copy(picked[t][:], act[t][:].indirect(take_sb[:]))

        def scatter(t):
            nc.vector.tensor_tensor(window[t][:].indirect(take_sb[:]), picked[t][:], wt_sb[t][:], MULT)

        for t in PLANE_ORDER[:3]:
            activate_and_gather(t)
        scatter(1)
        nc.sync.dma_start(out=wide[:, cols(1, S)], in_=window[1][:])

        w2s = sb.tile([P, H * PACK], BF16, name="w2s", align_bytes=64)
        for t in range(PACK):
            cast_first_layer(nc.scalar.copy, "w2", t, w2s[:, cols(t, P * PACK)])
        w2q = mx_operand("w2q", H)
        quantize(w2q[0][:], w2q[1][:], w2s[:])
        activate_and_gather(0)
        scatter(2)
        nc.sync.dma_start(out=wide[:, cols(2, S)], in_=window[2][:])
        scatter(3)

        z2s = sb.tile([P, S * PACK], BF16, name="z2s", align_bytes=64)
        for c in range(4):
            acc = bank((5 + c) % 8, [P, PACK, QUARTER], "y2_%d" % c)
            for t in range(PACK):
                mm(acc[:, t, :], w2q, cols(t, P), xq, cols(c, QUARTER), True, True)
            nc.scalar.activation(
                out=z2s[:, cols(c, QUARTER * PACK)].rearrange("p (n t) -> p n t", t=PACK),
                in_=acc[:].rearrange("p t n -> p n t"),
                func=GELU,
                bias=bias0[:],
            )

        second = {}
        staged_w = {}
        for name in ("w4", "w3"):
            staged_w[name] = sb.tile([P, N * PACK], BF16, name=name + "s", align_bytes=64)
            second[name] = mx_operand(name + "q", N)

        def cast_second_layer(name):
            for m in range(4):
                interleave(nc.scalar.copy, staged_w[name][:, cols(m, P * PACK)], raw[name][:, :, cols(m, P)])

        def quantize_w3(h):
            width = N // 2
            quantize(
                second["w3"][0][:, cols(h, width)],
                second["w3"][1][:, cols(h, width)],
                staged_w["w3"][:, cols(h, width * PACK)],
            )

        z2q = mx_operand("z2q", S)
        quantize(z2q[0][:], z2q[1][:], z2s[:])
        cast_second_layer("w4")
        quantize(second["w4"][0][:], second["w4"][1][:], staged_w["w4"][:])
        result = {}
        for h in range(2):
            for m in range(4):
                result[h, m] = bank((1 + 4 * h + m) % 8, [P, HALF], "out%d_%d" % (h, m))
                mm(result[h, m][:], second["w4"], cols(m, P), z2q, cols(h, HALF), True, False)

        nc.scalar.copy(out=wide[:, cols(3, S)], in_=window[3][:])
        scatter(0)
        cast_second_layer("w3")

        planes = wide[:].rearrange("p (t c) -> p t c", t=PACK)
        zq = mx_operand("zq", S)
        zs = [sb.tile([P, HALF * PACK], BF16, name="zs%d" % h, align_bytes=64) for h in range(2)]
        interleave(nc.vector.tensor_copy, zs[0][:], planes[:, :, 0:HALF])
        interleave(nc.scalar.copy, zs[1][:], planes[:, :, HALF:S])
        quantize_w3(0)
        quantize(zq[0][:, cols(0, HALF)], zq[1][:, cols(0, HALF)], zs[0][:])
        quantize_w3(1)
        quantize(zq[0][:, cols(1, HALF)], zq[1][:, cols(1, HALF)], zs[1][:])
        done = [sb.tile([P, S], F32, name="done%d" % m) for m in range(4)]
        for h, order in ((0, (0, 1, 2, 3)), (1, (2, 3, 0, 1))):
            for m in order:
                mm(result[h, m][:], second["w3"], cols(m, P), zq, cols(h, HALF), False, True)
                if m % 2 == 0:
                    nc.scalar.copy(out=done[m][:, cols(h, HALF)], in_=result[h, m][:])
                else:
                    nc.vector.tensor_copy(out=done[m][:, cols(h, HALF)], in_=result[h, m][:])
                if m < 2:
                    nc.sync.dma_start(out=out[cols(m, P), cols(h, HALF)], in_=done[m][:, cols(h, HALF)])
                elif h == 1:
                    nc.sync.dma_start(out=out[cols(m, P), :], in_=done[m][:])
